import numpy as np, ml_dtypes
CORES = [3,11,19,27,35,43,51,59]
N = 8
import mx_ref
BF = ml_dtypes.bfloat16
def cols(t, e):
    v = np.concatenate([t.reshape(128, -1, 4), np.zeros((128, 1, 4), BF)], axis=1)
    return np.ascontiguousarray(v[:, e]).reshape(128, -1)
def f(rng, *shape):
    return mx_ref.flush((rng.standard_normal(shape, dtype=np.float32) * np.exp2(rng.integers(-2, 3, shape[:-1] + (1,)))).astype(BF))
def wide(rng, *shape, cols=0):
    v = rng.standard_normal(shape, dtype=np.float32) * np.exp2(rng.integers(-12, 13, shape)).astype(np.float32)
    if cols: v *= np.repeat(np.exp2(rng.integers(-cols, cols + 1, shape[:-2] + (1, shape[-1] // 4))) * (rng.random(shape[:-2] + (1, shape[-1] // 4)) > 0.0625), 4, axis=-1).astype(np.float32)
    return mx_ref.flush(v.astype(BF))
T, K, O = 512, 128, 3
def setup_inputs(rng):
    u = np.zeros((128, 512), BF); u[:, :4] = f(rng, 128, 4)
    return {"x": f(rng, N, 128, 4 * T), "u": np.stack([u] * N), "w": f(rng, N, 128, 512 * O)}
def signs(d):
    return np.where(d["u"][0][:, :4].astype(np.float32) < 0, -1, 1).astype(np.float32)
def blocks(rng, n):
    return np.repeat(rng.permutation(16) < n, 8)
def plant(rng, d, n):
    for s in range(N):
        v = d["x"][s].astype(np.float32).reshape(128, T, 4)
        k = rng.permutation(T)[:n[s]]
        v[:, k] = np.abs(v[:, k]) * signs(d)[:, None] * np.float32(8)
        d["x"][s] = v.reshape(128, -1).astype(BF)
    return d
def setup_inputs_one(rng):
    d = setup_inputs(rng); return plant(rng, d, np.where(np.arange(N) == rng.integers(0, N), K, 0))
def setup_inputs_zeros(rng):
    d = setup_inputs(rng); m = blocks(rng, 2)
    d["u"][:, ~m] = 0
    k = rng.permutation(N * T); g = np.full(N * T, -1, np.float32)
    g[k[:K // 3]] = 1; g[k[K // 3:2 * (K // 3)]] = 0
    v = np.abs(d["x"][:, m].astype(np.float32)).reshape(N, -1, T, 4)
    d["x"][:, m] = (v * signs(d)[m][:, None] * g.reshape(N, 1, T, 1)).reshape(N, -1, 4 * T).astype(BF)
    return d
def setup_inputs_few(rng):
    d = setup_inputs(rng); p = rng.permutation(N); g = p[N - N // 2:]
    d["x"][g] = (-np.abs(d["x"][g].astype(np.float32)) * np.tile(signs(d), (1, T))).astype(BF)
    n = np.zeros(N, int); n[p[:2]] = [K * 3 // 5, K - K * 3 // 5]
    return plant(rng, d, n)
def setup_inputs_ties(rng):
    d = setup_inputs(rng); b = f(rng, 128, 4 * 80); m = blocks(rng, 4)
    d["u"][:, m] = 0
    d["x"] = np.stack([cols(b, rng.permutation(np.arange(T) % 80)) for r in range(N)])
    d["x"][:, m] = f(rng, N, 32, 4 * T); return d
def setup_inputs_spread(rng):
    d = setup_inputs(rng); d["x"] = wide(rng, N, 128, 4 * T, cols=8); return d
def check_inputs(d):
    b = []
    u = d["u"].astype(np.float32)
    if (u != u[:1]).any(): b.append("u_same")
    if (u[:, :, 4:] != 0).any(): b.append("u_zero")
    return b
def reference(x, u, w):
    s = np.stack([mx_ref.matmul(mx_ref.quantize(u[r]), mx_ref.quantize(x[r]))[0] for r in range(N)]).reshape(-1) + np.float32(0.0)
    best = np.lexsort((np.arange(N * T), -s))[:K]
    V = mx_ref.quantize(cols(np.concatenate(list(x), axis=1), best))
    y = np.zeros((N, 128, O * K), np.float32)
    for r in range(N):
        for o in range(O): y[r][:, K * o:K * o + K] = mx_ref.matmul(mx_ref.quantize(np.ascontiguousarray(w[r][:, 512 * o:512 * o + 512])), V)
    who = np.stack([best // T, best % T]).astype(np.float32)
    return {"y": y, "id": np.stack([who] * N)}

from concourse.bass import DstId, RemoteDMATransfer
from concourse.mybir import dt, AluOpType as A, ActivationFunctionType as F, AxisListType

N, NB, K2, BIG = 8, 16, 32, 1.0e29
SCRATCH = {"psb": ("psum", [128, 2048], "float32"), "pss": ("psum", [128, 2048], "float32")}
for _d, _l in (("float8_e4m3fn_x4", "xq 512 uq 128 ur 128 wq 384 snd1 128 land1 128 snd2 32 land2 256"),
               ("uint8", "xs 512 us 128 urs 128 ws 384 snd1s 128 land1s 128 snd2s 32 land2s 256"),
               ("bfloat16", "xb 2048 ub 512 wb 1536 k2 96 k3 256 jb 4 g1 2560 r1 1280 g2 256 g3 1024 r3 512 oh3 512 ot3 512"),
               ("uint16", "zoff 8 off1 8 off2 2 off3 8"), ("int32", "l2 3 i2x 2 vg 128 wi 128 ji 128"),
               ("float32", "z32 32 zt 128 tri 128 on8 8 m8a 8 m8 8 sc1 4 st1 512 qa1 8 qb1 8 l1 8 lid 8 hid1 8 idl 32 sc2 1 st2 128 r2 128 m9 9 vp 1"
                " oh2 96 ot2 96 p2 3 qa2 3 qb2 3 vs 1 hid2 1 vl 32 xr 256 idr 256 idc 2 tie 512 sc3 2 st3 512 qa3 8 qb3 8 l3 8 ysb 768 yo 384 wf 128 jf 128")):
    _w = _l.split()
    for _i in range(0, len(_w), 2):
        SCRATCH[_w[_i]] = ("sbuf", [128, int(_w[_i + 1])], _d)
for _n, _k in (("krow", 32), ("oh1", 128), ("ot1", 128), ("sm1", 64), ("sm3", 32)):
    SCRATCH[_n] = ("sbuf", [128, 8, _k], "bfloat16")
SEMAPHORES = "vec sca ten pool du dx0 dx1 dx2 dx3 dw a1 a2 n1 n2 h1 h2 loc dy0 dy1 dy2 di0 di1".split()


def helper_of(core, T, topo):
    c = [h for h in topo.cores_of(core) if T.rank_of(h) is None and all(topo.may_write(h, d) for d in T.cores)]
    return sorted(c, key=lambda h: (topo.die(h) != topo.die(core), h))[0]


def near_engines(core, h, T, topo):
    far = [d for d in T.cores if d != core]
    return [e for e in topo.engines(core, h) if e not in topo.engines(core, far[0])][0:4]


def slot2(r):
    return 4 * (r % 2) + r // 2


def to_all(g, core, r, first, sem, src, dst, T, topo):
    tr = []
    for b in range(1, N):
        d = T.cores[(r + b) % N]
        rid, pid = topo.addr(d)[0:2]
        tr.append(RemoteDMATransfer(dst_ids=[DstId(rid=rid, pnc=pid)], dma_engine_mask=1 << topo.engines(core, d)[b - 1 + first], remote_sem=T.sem[sem], src=src(b), dst=dst))
    g.remote_dma_fused(tr, local_sem=T.sem.loc)


def hand_on(g, core, r, T, topo):
    n = len(near_engines(T.cores[r], core, T, topo))
    g.wait_ge(T.sem.h1, n)
    to_all(g, core, r, 0, "n1", lambda b: T.hid1[:, b:b + 1], T.idl[:, 4 * r:4 * r + 1], T, topo)
    g.wait_ge(T.sem.h2, n)
    to_all(g, core, r, 0, "n2", lambda b: T.hid2[:], T.vl[:, 4 * slot2(r):4 * slot2(r) + 1], T, topo)
    g.wait_ge(T.sem.loc, 2 * (N - 1))


def rank_program(g, core, T, topo):
    S, rank = T.sem, T.rank_of(core)
    if rank is None:
        for r in range(N):
            if helper_of(T.cores[r], T, topo) == core:
                hand_on(g, core, r, T, topo)
        return
    q = {"vec": g.vector, "sca": g.scalar, "ten": g.tensor, "pool": g, "sync": g.sync}
    v = g.vector
    ops = {"copy": v.tensor_copy, "tt": v.tensor_tensor, "ts": v.tensor_scalar, "red": v.tensor_reduce, "scan": v.tensor_tensor_scan,
           "tr": v.transpose, "set": v.memset, "qz": v.quantize_mx}
    cnt, seen = {}, {}

    def need(e, toks):
        best = {}
        for s, n in toks:
            best[s] = max(best.get(s, 0), n)
        for s in best:
            if seen.get((e, s), 0) < best[s]:
                q[e].wait_ge(S[s], best[s])
                seen[(e, s)] = best[s]

    def done(e, ins):
        cnt[e] = cnt.get(e, 0) + 1
        ins.then_inc(S[e], 1)
        return (e, cnt[e])

    def V(toks, name, *a):
        need("vec", toks)
        return done("vec", ops[name](*a))

    def ACT(toks, *a, **k):
        need("sca", toks)
        return done("sca", g.scalar.activation(*a, **k))

    def MM(toks, out, l, r):
        need("ten", toks)
        return done("ten", g.tensor.matmul_mx(out, l[0], l[1], r[0], r[1], True, True))

    def P(*a):
        return done("pool", g.affine_select(*a))

    def IOTA(*a):
        return done("pool", g.iota(*a, allow_small_or_imprecise_dtypes=True))

    def dma(e, toks, out, in_, sem):
        need(e, toks)
        q[e].dma_start(out, in_).then_inc(S[sem], 16)
        return (sem, 16)

    def u32(ap):
        return ap.bitcast(dt.uint32)

    def c128(i, w=128):
        return slice(w * i, w * i + w)

    du = dma("sca", [], T.ub[:], T.u[:], "du")
    dx = [dma(("sync", "sca")[i % 2], [], T.xb[:, c128(i, 512)], T.x[:, c128(i, 512)], "dx%d" % i) for i in range(4)]
    dw = dma("sync", [], T.wb[:], T.w[:], "dw")

    c_zoff = V([], "set", T.zoff[:], 0)
    c_zt = V([], "set", T.zt[:], 0.0)
    c_on = V([], "set", T.on8[:], 1.0)
    c_z32 = V([], "set", T.z32[:], 0.0)
    need("pool", [c_zt, c_on])
    c_tri = P(T.tri[:], T.zt[:], [[-1, 128]], A.is_gt, BIG, 0, 1)
    IOTA(T.jb[:], [[128, 4]], -256, 1)
    c_kr = IOTA(T.krow[:], [[1, 8], [0, 2], [8, 16]], 0, 0)
    c_ma = P(T.m8a[:], T.on8[:], [[-16, 8]], A.is_ge, 0.0, 0, 1)
    need("pool", [c_ma])
    P(T.m8[:], T.m8a[:], [[16, 8]], A.is_ge, 0.0, 15, -1)
    IOTA(T.m9[:, 8:9], [[0, 1]], 0, 1)
    IOTA(T.k2[:, 0:64], [[16, 2], [0, 2], [1, 16]], 0, 0)
    IOTA(T.k2[:, 64:96], [[1, 32]], 0, 0)
    c_k3 = IOTA(T.k3[:], [[16, 8], [0, 2], [1, 16]], 0, 0)

    t = V([du], "qz", T.uq[:], T.us[:], T.ub[:])
    c_ur = V([t, c_zoff], "copy", u32(T.ur[:]), u32(T.uq[:]).indirect(T.zoff[:]))
    c_us = ACT([t, c_zoff], T.urs[:], T.us[:].indirect(T.zoff[:]), F.Copy)
    U = (T.ur[:], T.urs[:])

    tq, tB, sc, st, rk, oh, last = {}, {}, {}, {}, {}, {}, {}

    def quant(i):
        X = (T.xq[:, c128(i)], T.xs[:, c128(i)])
        tq[i] = V([dx[i]], "qz", X[0], X[1], T.xb[:, c128(i, 512)])
        t = MM([tq[i], c_ur, c_us], T.pss[:, 512 * i:512 * i + 128], X, U)
        tB[i] = MM([], T.psb[:, 512 * i:512 * i + 128], U, X)
        sc[i] = ACT([t], T.sc1[:, i:i + 1], T.pss[:, 512 * i:512 * i + 1], F.Copy)
        st[i] = ACT([sc[i], c_tri], T.st1[:, c128(i)], T.tri[:], F.Identity, bias=T.sc1[:, i:i + 1])

    def blocks(*ci):
        for c, i in ci:
            last[c] = V([tB[i], sc[c]], "ts", T.g1[:, 640 * c + 128 * i:640 * c + 128 * i + 128], T.psb[:, 512 * i:512 * i + 128], T.sc1[:, c:c + 1], None, A.is_ge if i < c else A.is_gt)

    def equal(c):
        last[c] = V([tB[c], st[c]], "tt", T.g1[:, 640 * c + 512:640 * c + 640], T.psb[:, 512 * c:512 * c + 128], T.st1[:, c128(c)], A.is_equal)

    def count(c):
        rk[c] = V([last[c]], "scan", T.r1[:, c128(c, 320)], T.g1[:, 640 * c:640 * c + 320], T.g1[:, 640 * c + 320:640 * c + 640], 0.0, A.add, A.add)

    quant(0)
    quant(1)
    blocks((0, 0), (0, 1), (1, 0), (1, 1))
    quant(2)
    equal(0)
    equal(1)
    blocks((0, 2), (1, 2), (2, 0), (2, 1), (2, 2))
    quant(3)
    equal(2)
    blocks((0, 3), (1, 3), (2, 3), (3, 0), (3, 1), (3, 2), (3, 3))
    for c in range(3):
        count(c)
    equal(3)
    count(3)
    free1 = [last[3]] + list(sc.values())
    for c in range(4):
        oh[c] = V([rk[c], c_kr], "ts", T.oh1[:, :, c128(c, 32)], T.krow[:], T.r1[:, 320 * c + 319:320 * c + 320], T.jb[:, c:c + 1], A.is_equal, A.mult)
    tr = [V(list(oh.values()), "tr", T.ot1[:, b, :], T.oh1[:, b, :]) for b in range(8)]
    sm = [V([tr[b]], "scan", T.sm1[:, b, :], T.ot1[:, b, 0:64], T.ot1[:, b, 64:128], 0.0, A.add, A.add) for b in range(8)]

    def fold(toks, src, qa, qb, dst):
        t0 = V(toks, "tt", qa[0:32, :], src(0), src(32), A.add)
        t1 = V(toks, "tt", qb[0:32, :], src(64), src(96), A.add)
        return [V([t0, t1], "tt", dst[a:a + 32, :], qa[0:32, :], qb[0:32, :], A.add) for a in (0, 32, 64, 96)]

    l1 = fold(sm, lambda a: T.sm1[a:a + 32, :, 63], T.qa1, T.qb1, T.l1)
    off1 = V(l1, "ts", T.off1[:], T.l1[:], 256.0, None, A.add)
    lid = ACT(l1, T.lid[:], T.l1[:], F.Identity, bias=65536.0 * rank + 32768.0, scale=128.0)
    me1 = c128(rank, NB)
    pc = V([off1], "copy", u32(T.snd1[:]), u32(T.xq[:]).indirect(T.off1[:]))
    psc = ACT([off1], T.snd1s[:], T.xs[:].indirect(T.off1[:]), F.Copy)
    oc = V([], "copy", u32(T.land1[:, me1]), u32(T.xq[:]).indirect(T.off1[:, 0:1]))
    osc = ACT([], T.land1s[:, me1], T.xs[:].indirect(T.off1[:, 0:1]), F.Copy)
    oid = ACT(l1, T.idl[:, 4 * rank:4 * rank + 1], T.l1[:, 0:1], F.Identity, bias=65536.0 * rank + 32768.0, scale=128.0)

    h = helper_of(core, T, topo)
    hrid, hpid = topo.addr(h)[0:2]
    near = near_engines(core, h, T, topo)

    def send(tok, out, in_, sem):
        need("pool", [tok])
        g.remote_dma(out, in_, S[sem], S.loc, hpid, hrid, sum(1 << e for e in near))

    send(lid, T.hid1[:], T.lid[:], "h1")
    need("pool", [pc])
    to_all(g, core, rank, 0, "a1", lambda b: T.snd1[:, c128(b, NB)].bitcast(dt.uint8), T.land1[:, me1].bitcast(dt.uint8), T, topo)
    need("pool", [psc])
    to_all(g, core, rank, 1, "a1", lambda b: T.snd1s[:, c128(b, NB)], T.land1s[:, me1], T, topo)

    wq = V([dw], "qz", T.wq[:], T.ws[:], T.wb[:])

    arr1 = [("a1", 14), oc, osc]
    L1 = (T.land1[:], T.land1s[:])
    t = MM(arr1 + free1, T.pss[:, 0:128], L1, U)
    tB2 = MM([], T.psb[:, 0:128], U, L1)
    sc2 = ACT([t], T.sc2[:], T.pss[:, 0:1], F.Copy)
    st2 = ACT([sc2], T.st2[:], T.tri[:], F.Identity, bias=T.sc2[:])
    V([tB2, sc2], "ts", T.g2[:, 0:128], T.psb[:, 0:128], T.sc2[:], None, A.is_gt)
    e2 = V([st2], "tt", T.g2[:, 128:256], T.psb[:, 0:128], T.st2[:], A.is_equal)
    t = V([("n1", 7), oid, c_k3], "tt", T.m9[:, 0:8], T.idl[:, 0:32:4], T.m8[:], A.mult)
    r2 = V([e2], "scan", T.r2[:], T.g2[:, 0:128], T.g2[:, 128:256], 0.0, A.add, A.add)
    vp = V([t], "red", T.vp[:], T.m9[:], AxisListType.X, A.add)
    t = V([r2, vp], "ts", T.oh2[:], T.k2[:], T.r2[:, 127:128], T.vp[:], A.is_equal, A.mult)
    t = V([t], "tr", T.ot2[:], T.oh2[:])
    p2 = [V([t], "red", T.p2[:, b:b + 1], T.ot2[:, c128(b, 32)], AxisListType.X, A.add) for b in range(3)]
    l2 = fold(p2, lambda a: T.p2[a:a + 32, :], T.qa2, T.qb2, T.l2)
    t = V(l2, "ts", T.i2x[:], T.l2[:, 0:2], 127, None, A.bitwise_and)
    vs = V(l2, "copy", T.vs[:], T.l2[:, 2:3])
    off2 = V([t], "copy", T.off2[:], T.i2x[:])
    b2 = slot2(rank)
    me2 = c128(b2, K2)
    pc = V([off2] + arr1, "copy", u32(T.snd2[:]), u32(T.land1[:]).indirect(T.off2[:]))
    psc = ACT([off2] + arr1, T.snd2s[:], T.land1s[:].indirect(T.off2[:]), F.Copy)
    oc2 = V([], "copy", u32(T.land2[:, me2]), u32(T.land1[:]).indirect(T.off2[:]))
    osc2 = ACT([], T.land2s[:, me2], T.land1s[:].indirect(T.off2[:]), F.Copy)
    ov = V(l2, "copy", T.vl[:, 4 * b2:4 * b2 + 1], T.l2[:, 2:3])
    send(vs, T.hid2[:], T.vs[:], "h2")
    need("pool", [pc])
    to_all(g, core, rank, 0, "a2", lambda b: T.snd2[:].bitcast(dt.uint8), T.land2[:, me2].bitcast(dt.uint8), T, topo)
    need("pool", [psc])
    to_all(g, core, rank, 1, "a2", lambda b: T.snd2s[:], T.land2s[:, me2], T, topo)

    xr = [ACT([("n2", 7), ov, c_z32], T.xr[:, c128(b, 32)], T.z32[:], F.Identity, bias=T.vl[:, 4 * b:4 * b + 1]) for b in range(8)]
    idc = [V([("n2", 7), ov], "copy", T.idc[32 * a:32 * a + 32, :], T.vl[32 * a:32 * a + 32, 4 * a:32:16]) for a in range(4)]
    idr = V(xr, "tr", T.idr[:], T.xr[:])
    tie = [V([idr] + idc, "ts", T.tie[:, c128(c, 256)], T.idr[:], T.idc[:, c:c + 1], BIG, A.is_ge, A.mult) for c in range(2)]

    arr2 = [("a2", 14), oc2, osc2]
    L2 = (T.land2[:], T.land2s[:])
    tS3 = [MM(arr2 + [e2, sc2] + free1, T.pss[:, 512 * c + 512:512 * c + 640], (T.land2[:, c128(c)], T.land2s[:, c128(c)]), U) for c in range(2)]
    b3 = T.psb[:, 512:768]
    tB3 = MM([], b3, U, L2)
    yps = [T.psb[:, 1024:1280], T.psb[:, 1536:1792], T.pss[:, 1536:1792]]
    tY = [MM([wq], yps[o], (T.wq[:, c128(o)], T.ws[:, c128(o)]), L2) for o in range(3)]
    sc3 = [ACT([tS3[c]], T.sc3[:, c:c + 1], T.pss[:, 512 * c + 512:512 * c + 513], F.Copy) for c in range(2)]
    st3 = [ACT([sc3[c], tie[c]], T.st3[:, c128(c, 256)], T.tie[:, c128(c, 256)], F.Identity, bias=T.sc3[:, c:c + 1]) for c in range(2)]
    ysb = [ACT([tY[o]], T.ysb[:, c128(o, 256)], yps[o], F.Copy) for o in range(3)]
    g3 = [V([tB3, sc3[c]], "ts", T.g3[:, 512 * c:512 * c + 256], b3, T.sc3[:, c:c + 1], None, A.is_gt) for c in range(2)]
    e3 = [V([st3[c]], "tt", T.g3[:, 512 * c + 256:512 * c + 512], b3, T.st3[:, c128(c, 256)], A.is_equal) for c in range(2)]
    r3 = [V([g3[c], e3[c]], "scan", T.r3[:, c128(c, 256)], T.g3[:, 512 * c:512 * c + 256], T.g3[:, 512 * c + 256:512 * c + 512], 0.0, A.add, A.add) for c in range(2)]
    oh3 = [V([r3[c]], "ts", T.oh3[:, c128(c, 256)], T.k3[:], T.r3[:, 256 * c + 255:256 * c + 256], T.jb[:, c + 2:c + 3], A.is_equal, A.mult) for c in range(2)]
    t = V(oh3, "tr", T.ot3[:], T.oh3[:])
    sm3 = [V([t], "scan", T.sm3[:, b, :], T.ot3[:, c128(b, 32)], T.ot3[:, 256 + 32 * b:288 + 32 * b], 0.0, A.add, A.add) for b in range(8)]
    l3 = fold(sm3, lambda a: T.sm3[a:a + 32, :, 31], T.qa3, T.qb3, T.l3)
    off3 = V(l3, "copy", T.off3[:], T.l3[:])
    y0 = V([off3] + ysb, "copy", T.yo[:, c128(0)], T.ysb[:, 0:256].indirect(T.off3[:]))
    y1 = ACT([off3] + ysb, T.yo[:, c128(1)], T.ysb[:, 256:512].indirect(T.off3[:]), F.Copy)
    y2 = ACT([], T.yo[:, c128(2)], T.ysb[:, 512:768].indirect(T.off3[:]), F.Copy)
    vg = V([], "copy", T.vg[:], T.idr[:].indirect(T.off3[:]))
    wi = V([vg], "ts", T.wi[0:1, :], T.vg[0:1, :], 16, None, A.arith_shift_right)
    ji = V([vg], "ts", T.ji[0:1, :], T.vg[0:1, :], 7, 511, A.arith_shift_right, A.bitwise_and)
    wf = V([wi], "copy", T.wf[0:1, :], T.wi[0:1, :])
    jf = V([ji], "copy", T.jf[0:1, :], T.ji[0:1, :])
    outs = [dma("sync", [y0], T.y[:, c128(0)], T.yo[:, c128(0)], "dy0"), dma("sync", [y1], T.y[:, c128(1)], T.yo[:, c128(1)], "dy1"),
            dma("sca", [y2], T.y[:, c128(2)], T.yo[:, c128(2)], "dy2"),
            dma("sync", [wf], T["id"][0:1, :], T.wf[0:1, :], "di0"), dma("sca", [jf], T["id"][1:2, :], T.jf[0:1, :], "di1")]
    need("pool", list(cnt.items()) + [("a1", 14), ("a2", 14), ("n1", 7), ("n2", 7), ("loc", 4 * (N - 1) + 2 * len(near)), du, dw] + dx + outs)
